import numpy as np
import ml_dtypes


def mxq(x, axis, fmt="e4m3"):
    dtype, down = {"e4m3": (ml_dtypes.float8_e4m3fn, 7), "e5m2": (ml_dtypes.float8_e5m2, 14)}[fmt]
    v = np.moveaxis(np.asarray(x, np.float32).astype(ml_dtypes.bfloat16).astype(np.float64), axis, -1)
    blocks = v.reshape(v.shape[:-1] + (-1, 32))
    amax = np.abs(blocks).max(-1, keepdims=True)
    byte = np.maximum(np.where(amax > 0, np.frexp(amax)[1] - 1 + 127, 0) - down, 1)
    scale = np.exp2(byte - 127.0)
    codes = (blocks / scale).astype(np.float32).astype(dtype).astype(np.float64)
    return np.moveaxis((codes * scale).reshape(v.shape), -1, axis)


WIDE = False


def mx_kscale(k):
    if not WIDE:
        return np.ones(k)
    levels = np.array([10, -10, 5, -5, 0])
    if k % 512:
        return np.exp2(np.random.permutation(np.resize(levels, k // 32))).repeat(32)
    a = np.empty((k // 512, 16))
    for p in range(k // 512):
        a[p, :8] = np.random.permutation(np.resize(levels, 8))
        for g in range(8):
            far = levels[np.abs(levels - a[p, g]) >= 10]
            a[p, g + 8] = far[np.random.randint(len(far))]
    return np.exp2(a.ravel()).repeat(32)


def f64(x):
    return np.asarray(x).astype(np.float64)


def striped(idx):
    return np.tile(np.asarray(idx).reshape(-1, 16).T, (8, 1)).astype(np.uint16)


def unstriped(offs):
    return offs[:16].T.reshape(-1).astype(np.int64)


def sigmoid(v):
    return 1.0 / (1.0 + np.exp(-v))


D, T, I, Q, M = 512, 2048, 512, 128, 2048


def setup_inputs():
    n = np.random.standard_normal
    idx = np.random.permutation(T)[:I]
    idx2 = np.random.permutation(T)[:I]
    idx3 = np.random.permutation(T)[:I]
    idx4 = np.random.permutation(M)[:I]
    fd = mx_kscale(D)
    return {
        "query": (n((D, Q)) * 1.0 / np.sqrt(D) * fd[:, None]).astype(np.float32),
        "keys": (n((D, T)) / fd[:, None]).astype(np.float32),
        "old": (np.random.uniform(0.0, 2.0, (Q, M))).astype(np.float32),
        "fade": (np.random.uniform(0.3, 0.9, (Q, 1))).astype(np.float32),
        "offs": striped(idx),
        "offs2": striped(idx2),
        "offs3": striped(idx3),
        "offs4": striped(idx4),
    }


def reference(query, keys, old, fade, offs, offs2, offs3, offs4):
    idx = unstriped(offs)
    idx2 = unstriped(offs2)
    idx3 = unstriped(offs3)
    idx4 = unstriped(offs4)
    lo3 = np.minimum(f64(keys)[:, idx], f64(keys)[:, idx2])
    hi3 = np.maximum(f64(keys)[:, idx], f64(keys)[:, idx2])
    zk = np.maximum(lo3, np.minimum(hi3, f64(keys)[:, idx3]))
    queryq = mxq(f64(query), 0, "e4m3")
    zkq = mxq(zk, 0, "e4m3")
    s = queryq.T @ zkq
    w = sigmoid(s)
    ws = w * 2.0
    wf = np.zeros((Q, M))
    wf[:, idx4] = ws
    y = f64(old) * f64(fade) + wf
    return y

@@ -1,0 +1,169 @@
+from contextlib import ExitStack
+
+import concourse.mybir as mybir
+
+D, T, I, Q, M = 512, 2048, 512, 128, 2048
+FLOPS = 2 * D * Q * I
+
+F32 = mybir.dt.float32
+BF16 = mybir.dt.bfloat16
+U32 = mybir.dt.uint32
+U16 = mybir.dt.uint16
+U8 = mybir.dt.uint8
+FP8X4 = mybir.dt.float8_e4m3fn_x4
+ALU = mybir.AluOpType
+ACT = mybir.ActivationFunctionType
+
+P = 128
+PACK = 4
+LINE = 4
+PER_COLUMN = 16
+QUARTER = I // 4
+HALF = I // 2
+STORE_WIDTHS = (256, 512, 512, 512, 256)
+
+
+def entries(offsets, first, count):
+    return offsets[:, first // PER_COLUMN : (first + count) // PER_COLUMN]
+
+
+def tile_attend_keymiddle_counts_lean_kernel(tc, query, keys, old, fade, offs, offs2, offs3, offs4, out):
+    nc = tc.nc
+    with ExitStack() as ctx:
+        sb = ctx.enter_context(tc.tile_pool(name="sb", bufs=1))
+        ps = ctx.enter_context(tc.psum_pool(name="ps", bufs=1))
+
+        list_a = sb.tile([P, I // PER_COLUMN], U16, name="list_a")
+        list_b = sb.tile([P, I // PER_COLUMN], U16, name="list_b")
+        list_c = sb.tile([P, I // PER_COLUMN], U16, name="list_c")
+        list_out = sb.tile([P, I // PER_COLUMN], U16, name="list_out")
+        planes = [sb.tile([P, T], F32, name=f"plane{t}") for t in range(PACK)]
+        key_rows = keys.rearrange("(p t) n -> t p n", t=PACK)
+        q_raw = sb.tile([P, PACK, Q], F32, name="q_raw")
+        old_sb = sb.tile([P, M], F32, name="old_sb")
+        fade_sb = sb.tile([P, 1], F32, name="fade_sb")
+
+        nc.sync.dma_start(planes[0][:], key_rows[0])
+        nc.sync.dma_start(list_a[:], offs)
+        nc.sync.dma_start(list_b[:], offs2)
+        nc.sync.dma_start(list_c[:], offs3)
+        for t in range(1, PACK):
+            nc.sync.dma_start(planes[t][:], key_rows[t])
+        nc.sync.dma_start(q_raw[:], query.rearrange("(p t) q -> p t q", t=PACK))
+        nc.sync.dma_start(list_out[:], offs4)
+        nc.sync.dma_start(fade_sb[:], fade)
+        nc.sync.dma_start(old_sb[:], old)
+
+        wf = sb.tile([P, M], F32, name="wf")
+        nc.vector.memset(wf[:], 0.0)
+
+        lo = sb.tile([P, PACK, I], F32, name="lo")
+        mid = sb.tile([P, PACK, I], F32, name="mid")
+
+        def gather(on_vector, dst, t, offsets, first, count):
+            src = planes[t][:].indirect(entries(offsets, first, count))
+            if on_vector:
+                nc.vector.tensor_copy(dst, src)
+            else:
+                nc.scalar.activation(dst, src, ACT.Copy)
+
+        for t in range(PACK - 1):
+            a = sb.tile([P, I], F32, name=f"a{t}")
+            b = sb.tile([P, I], F32, name=f"b{t}")
+            c = sb.tile([P, I], F32, name=f"c{t}")
+            hi = sb.tile([P, I], F32, name=f"hi{t}")
+            gather(False, a[:], t, list_a, 0, I)
+            if t < PACK - 2:
+                gather(True, b[:], t, list_b, 0, I)
+            else:
+                gather(True, b[:, :HALF], t, list_b, 0, HALF)
+                gather(False, b[:, HALF:], t, list_b, HALF, HALF)
+            gather(False, c[:], t, list_c, 0, I)
+            nc.vector.tensor_tensor(hi[:], a[:], b[:], ALU.max)
+            nc.vector.tensor_tensor(lo[:, t, :], a[:], b[:], ALU.min)
+            nc.vector.tensor_tensor(mid[:, t, :], hi[:], c[:], ALU.min)
+
+        q_bf = sb.tile([P, Q, PACK], BF16, name="q_bf", align_bytes=64)
+        q_codes = sb.tile([P, Q], U32, name="q_codes", align_bytes=64)
+        q_scales = sb.tile([P, Q], U8, name="q_scales", align_bytes=64)
+        nc.vector.tensor_copy(
+            q_bf[:].rearrange("p (c i) t -> p c t i", i=LINE),
+            q_raw[:].rearrange("p t (c i) -> p c t i", i=LINE),
+        )
+        nc.vector.quantize_mx(q_codes[:].bitcast(FP8X4), q_scales[:], q_bf[:].rearrange("p q t -> p (q t)"))
+
+        last = PACK - 1
+        w_first = sb.tile([P, HALF], F32, name="w_first")
+        w_rest = [sb.tile([P, QUARTER], F32, name=f"w{j}") for j in (2, 3)]
+        w_of = [w_first[:, :QUARTER], w_first[:, QUARTER:], w_rest[0][:], w_rest[1][:]]
+        zk = [sb.tile([P, QUARTER, PACK], BF16, name=f"zk{j}", align_bytes=64) for j in range(4)]
+        his = [sb.tile([P, QUARTER], F32, name=f"hi_last{j}") for j in range(4)]
+        abc = [[sb.tile([P, QUARTER], F32, name=f"{n}_last{j}") for n in "abc"] for j in range(4)]
+
+        def cols(j):
+            return slice(j * QUARTER, (j + 1) * QUARTER)
+
+        def gathers(j):
+            for dst, offsets in zip(abc[j], (list_a, list_b, list_c)):
+                gather(False, dst[:], last, offsets, j * QUARTER, QUARTER)
+
+        def upper(j):
+            nc.vector.tensor_tensor(his[j][:], abc[j][0][:], abc[j][1][:], ALU.max)
+
+        def lower(j):
+            nc.vector.tensor_tensor(lo[:, last, cols(j)], abc[j][0][:], abc[j][1][:], ALU.min)
+
+        def cap(j):
+            nc.vector.tensor_tensor(mid[:, last, cols(j)], his[j][:], abc[j][2][:], ALU.min)
+
+        def middle(j):
+            nc.vector.tensor_tensor(
+                zk[j][:].rearrange("p (c i) t -> p c t i", i=LINE),
+                lo[:, :, cols(j)].rearrange("p t (c i) -> p c t i", i=LINE),
+                mid[:, :, cols(j)].rearrange("p t (c i) -> p c t i", i=LINE),
+                ALU.max,
+            )
+
+        def weigh(j):
+            codes = sb.tile([P, QUARTER], U32, name=f"k_codes{j}", align_bytes=64)
+            scales = sb.tile([P, QUARTER], U8, name=f"k_scales{j}", align_bytes=64)
+            nc.vector.quantize_mx(codes[:].bitcast(FP8X4), scales[:], zk[j][:].rearrange("p i t -> p (i t)"))
+            s = ps.tile([P, QUARTER], F32, name=f"s{j}")
+            nc.tensor.matmul_mx(
+                s[:],
+                lhsT=q_codes[:].bitcast(FP8X4),
+                lhsT_scale=q_scales[:],
+                rhs=codes[:].bitcast(FP8X4),
+                rhs_scale=scales[:],
+                start=True,
+                stop=True,
+            )
+            nc.scalar.activation(w_of[j], s[:], ACT.Sigmoid)
+
+        for j in range(4):
+            gathers(j)
+        upper(0)
+        lower(0)
+        cap(0)
+        for j in range(4):
+            if j < 3:
+                upper(j + 1)
+            middle(j)
+            if j < 3:
+                lower(j + 1)
+            weigh(j)
+            if j < 3:
+                cap(j + 1)
+            if j == 1:
+                nc.scalar.activation(wf[:].indirect(entries(list_out, 0, HALF)), w_first[:], ACT.Copy, scale=2.0)
+        for j in (2, 3):
+            nc.vector.tensor_tensor(wf[:].indirect(entries(list_out, j * QUARTER, QUARTER)), w_of[j], w_of[j], ALU.add)
+
+        first = 0
+        for n, width in enumerate(STORE_WIDTHS):
+            span = slice(first, first + width)
+            res = sb.tile([P, width], F32, name=f"res{n}")
+            nc.vector.scalar_tensor_tensor(res[:], old_sb[:, span], fade_sb[:], wf[:, span], ALU.mult, ALU.add)
+            queue = nc.sync if n % 2 == 0 else nc.scalar
+            queue.dma_start(out[:, span], res[:])
+            first = first + width

@@ -16,11 +16,12 @@ ACT = mybir.ActivationFunctionType
 
 P = 128
 PACK = 4
-LINE = 4
+LINE = 2
 PER_COLUMN = 16
 QUARTER = I // 4
 HALF = I // 2
 STORE_WIDTHS = (256, 512, 512, 512, 256)
+VECTOR_SHARE_OF_B = (512, 512, 256)
 
 
 def entries(offsets, first, count):
@@ -54,6 +55,11 @@ def tile_attend_keymiddle_counts_lean_kernel(tc, query, keys, old, fade, offs, o
         nc.sync.dma_start(fade_sb[:], fade)
         nc.sync.dma_start(old_sb[:], old)
 
+        warm_in = sb.tile([P, 1], F32, name="warm_in")
+        warm_out = sb.tile([P, 1], F32, name="warm_out")
+        nc.vector.memset(warm_in[:], 0.0)
+        nc.scalar.activation(warm_out[:], warm_in[:], ACT.Sigmoid)
+
         wf = sb.tile([P, M], F32, name="wf")
         nc.vector.memset(wf[:], 0.0)
 
@@ -73,62 +79,51 @@ def tile_attend_keymiddle_counts_lean_kernel(tc, query, keys, old, fade, offs, o
             c = sb.tile([P, I], F32, name=f"c{t}")
             hi = sb.tile([P, I], F32, name=f"hi{t}")
             gather(False, a[:], t, list_a, 0, I)
-            if t < PACK - 2:
-                gather(True, b[:], t, list_b, 0, I)
-            else:
-                gather(True, b[:, :HALF], t, list_b, 0, HALF)
-                gather(False, b[:, HALF:], t, list_b, HALF, HALF)
+            share = VECTOR_SHARE_OF_B[t]
+            if share:
+                gather(True, b[:, :share], t, list_b, 0, share)
+            if share < I:
+                gather(False, b[:, share:], t, list_b, share, I - share)
             gather(False, c[:], t, list_c, 0, I)
             nc.vector.tensor_tensor(hi[:], a[:], b[:], ALU.max)
             nc.vector.tensor_tensor(lo[:, t, :], a[:], b[:], ALU.min)
             nc.vector.tensor_tensor(mid[:, t, :], hi[:], c[:], ALU.min)
 
-        q_bf = sb.tile([P, Q, PACK], BF16, name="q_bf", align_bytes=64)
-        q_codes = sb.tile([P, Q], U32, name="q_codes", align_bytes=64)
-        q_scales = sb.tile([P, Q], U8, name="q_scales", align_bytes=64)
-        nc.vector.tensor_copy(
-            q_bf[:].rearrange("p (c i) t -> p c t i", i=LINE),
-            q_raw[:].rearrange("p t (c i) -> p c t i", i=LINE),
-        )
-        nc.vector.quantize_mx(q_codes[:].bitcast(FP8X4), q_scales[:], q_bf[:].rearrange("p q t -> p (q t)"))
-
         last = PACK - 1
-        w_first = sb.tile([P, HALF], F32, name="w_first")
-        w_rest = [sb.tile([P, QUARTER], F32, name=f"w{j}") for j in (2, 3)]
-        w_of = [w_first[:, :QUARTER], w_first[:, QUARTER:], w_rest[0][:], w_rest[1][:]]
-        zk = [sb.tile([P, QUARTER, PACK], BF16, name=f"zk{j}", align_bytes=64) for j in range(4)]
-        his = [sb.tile([P, QUARTER], F32, name=f"hi_last{j}") for j in range(4)]
-        abc = [[sb.tile([P, QUARTER], F32, name=f"{n}_last{j}") for n in "abc"] for j in range(4)]
+        halves = [slice(0, HALF), slice(HALF, I)]
+        abc = [[sb.tile([P, HALF], F32, name=f"{x}_last{h}") for x in "abc"] for h in range(2)]
+        hi_first = sb.tile([P, HALF], F32, name="hi_first")
+        his = [hi_first[:], sb.tile([P, HALF], F32, name="hi_second")[:]]
 
-        def cols(j):
-            return slice(j * QUARTER, (j + 1) * QUARTER)
+        def gathers(h):
+            for dst, offsets in zip(abc[h], (list_a, list_b, list_c)):
+                gather(False, dst[:], last, offsets, h * HALF, HALF)
 
-        def gathers(j):
-            for dst, offsets in zip(abc[j], (list_a, list_b, list_c)):
-                gather(False, dst[:], last, offsets, j * QUARTER, QUARTER)
+        def upper(h):
+            nc.vector.tensor_tensor(his[h], abc[h][0][:], abc[h][1][:], ALU.max)
 
-        def upper(j):
-            nc.vector.tensor_tensor(his[j][:], abc[j][0][:], abc[j][1][:], ALU.max)
+        def lower(h):
+            nc.vector.tensor_tensor(lo[:, last, halves[h]], abc[h][0][:], abc[h][1][:], ALU.min)
 
-        def lower(j):
-            nc.vector.tensor_tensor(lo[:, last, cols(j)], abc[j][0][:], abc[j][1][:], ALU.min)
+        def cap(h):
+            nc.vector.tensor_tensor(mid[:, last, halves[h]], his[h], abc[h][2][:], ALU.min)
 
-        def cap(j):
-            nc.vector.tensor_tensor(mid[:, last, cols(j)], his[j][:], abc[j][2][:], ALU.min)
-
-        def middle(j):
+        def middle(first, count):
+            zk = sb.tile([P, count, PACK], BF16, name=f"zk{first}", align_bytes=64)
+            span = slice(first, first + count)
             nc.vector.tensor_tensor(
-                zk[j][:].rearrange("p (c i) t -> p c t i", i=LINE),
-                lo[:, :, cols(j)].rearrange("p t (c i) -> p c t i", i=LINE),
-                mid[:, :, cols(j)].rearrange("p t (c i) -> p c t i", i=LINE),
+                zk[:].rearrange("p (c i) t -> p c t i", i=LINE),
+                lo[:, :, span].rearrange("p t (c i) -> p c t i", i=LINE),
+                mid[:, :, span].rearrange("p t (c i) -> p c t i", i=LINE),
                 ALU.max,
             )
+            return zk
 
-        def weigh(j):
-            codes = sb.tile([P, QUARTER], U32, name=f"k_codes{j}", align_bytes=64)
-            scales = sb.tile([P, QUARTER], U8, name=f"k_scales{j}", align_bytes=64)
-            nc.vector.quantize_mx(codes[:].bitcast(FP8X4), scales[:], zk[j][:].rearrange("p i t -> p (i t)"))
-            s = ps.tile([P, QUARTER], F32, name=f"s{j}")
+        def score(zk, first, count):
+            codes = sb.tile([P, count], U32, name=f"k_codes{first}", align_bytes=64)
+            scales = sb.tile([P, count], U8, name=f"k_scales{first}", align_bytes=64)
+            nc.vector.quantize_mx(codes[:].bitcast(FP8X4), scales[:], zk[:].rearrange("p i t -> p (i t)"))
+            s = ps.tile([P, count], F32, name=f"s{first}")
             nc.tensor.matmul_mx(
                 s[:],
                 lhsT=q_codes[:].bitcast(FP8X4),
@@ -138,26 +133,36 @@ def tile_attend_keymiddle_counts_lean_kernel(tc, query, keys, old, fade, offs, o
                 start=True,
                 stop=True,
             )
-            nc.scalar.activation(w_of[j], s[:], ACT.Sigmoid)
+            return s
 
-        for j in range(4):
-            gathers(j)
+        gathers(0)
+        q_bf = sb.tile([P, Q, PACK], BF16, name="q_bf", align_bytes=64)
+        q_codes = sb.tile([P, Q], U32, name="q_codes", align_bytes=64)
+        q_scales = sb.tile([P, Q], U8, name="q_scales", align_bytes=64)
+        nc.scalar.copy(
+            q_bf[:].rearrange("p (c i) t -> p c t i", i=LINE),
+            q_raw[:].rearrange("p t (c i) -> p c t i", i=LINE),
+        )
+        gathers(1)
         upper(0)
         lower(0)
         cap(0)
-        for j in range(4):
-            if j < 3:
-                upper(j + 1)
-            middle(j)
-            if j < 3:
-                lower(j + 1)
-            weigh(j)
-            if j < 3:
-                cap(j + 1)
-            if j == 1:
-                nc.scalar.activation(wf[:].indirect(entries(list_out, 0, HALF)), w_first[:], ACT.Copy, scale=2.0)
-        for j in (2, 3):
-            nc.vector.tensor_tensor(wf[:].indirect(entries(list_out, j * QUARTER, QUARTER)), w_of[j], w_of[j], ALU.add)
+        nc.vector.quantize_mx(q_codes[:].bitcast(FP8X4), q_scales[:], q_bf[:].rearrange("p q t -> p (q t)"))
+        zk_first = middle(0, HALF)
+        upper(1)
+        s_first = score(zk_first, 0, HALF)
+        w_first = sb.tile([P, HALF], F32, name="w_first")
+        nc.scalar.activation(w_first[:], s_first[:], ACT.Sigmoid)
+        nc.scalar.activation(wf[:].indirect(entries(list_out, 0, HALF)), w_first[:], ACT.Copy, scale=2.0)
+        lower(1)
+        cap(1)
+        quarters = (HALF, HALF + QUARTER)
+        zks = [middle(first, QUARTER) for first in quarters]
+        scores = [score(zk, first, QUARTER) for zk, first in zip(zks, quarters)]
+        for s, first in zip(scores, quarters):
+            w = sb.tile([P, QUARTER], F32, name=f"w{first}")
+            nc.scalar.activation(w[:], s[:], ACT.Sigmoid)
+            nc.vector.tensor_tensor(wf[:].indirect(entries(list_out, first, QUARTER)), w[:], w[:], ALU.add)
 
         first = 0
         for n, width in enumerate(STORE_WIDTHS):

@@ -15,17 +15,27 @@ ALU = mybir.AluOpType
 ACT = mybir.ActivationFunctionType
 
 P = 128
-PACK = 4
-LINE = 2
+PLANES = 4
+LAST = PLANES - 1
+RUN = 4
 PER_COLUMN = 16
-QUARTER = I // 4
 HALF = I // 2
-STORE_WIDTHS = (256, 512, 512, 512, 256)
-VECTOR_SHARE_OF_B = (512, 512, 256)
+QUARTERS = 4
+QUARTER = I // QUARTERS
+VECTOR_SLOTS = (512, 512, 256)
+STORE_WIDTHS = (256, 512, 512, 384, 256, 128)
 
 
 def entries(offsets, first, count):
     return offsets[:, first // PER_COLUMN : (first + count) // PER_COLUMN]
+
+
+def planes_in_runs(planes):
+    return planes.rearrange("p t (c i) -> p c t i", i=RUN)
+
+
+def words_in_runs(words):
+    return words.rearrange("p (c i) t -> p c t i", i=RUN)
 
 
 def tile_attend_keymiddle_counts_lean_kernel(tc, query, keys, old, fade, offs, offs2, offs3, offs4, out):
@@ -38,19 +48,20 @@ def tile_attend_keymiddle_counts_lean_kernel(tc, query, keys, old, fade, offs, o
         list_b = sb.tile([P, I // PER_COLUMN], U16, name="list_b")
         list_c = sb.tile([P, I // PER_COLUMN], U16, name="list_c")
         list_out = sb.tile([P, I // PER_COLUMN], U16, name="list_out")
-        planes = [sb.tile([P, T], F32, name=f"plane{t}") for t in range(PACK)]
-        key_rows = keys.rearrange("(p t) n -> t p n", t=PACK)
-        q_raw = sb.tile([P, PACK, Q], F32, name="q_raw")
+        key_planes = [sb.tile([P, T], F32, name=f"key_plane{t}") for t in range(PLANES)]
+        key_rows = keys.rearrange("(p t) n -> t p n", t=PLANES)
+        q_planes = sb.tile([P, PLANES, Q], F32, name="q_planes")
         old_sb = sb.tile([P, M], F32, name="old_sb")
         fade_sb = sb.tile([P, 1], F32, name="fade_sb")
 
-        nc.sync.dma_start(planes[0][:], key_rows[0])
+        nc.sync.dma_start(key_planes[0][:], key_rows[0])
         nc.sync.dma_start(list_a[:], offs)
         nc.sync.dma_start(list_b[:], offs2)
         nc.sync.dma_start(list_c[:], offs3)
-        for t in range(1, PACK):
-            nc.sync.dma_start(planes[t][:], key_rows[t])
-        nc.sync.dma_start(q_raw[:], query.rearrange("(p t) q -> p t q", t=PACK))
+        for t in range(1, LAST):
+            nc.sync.dma_start(key_planes[t][:], key_rows[t])
+        nc.sync.dma_start(q_planes[:], query.rearrange("(p t) q -> p t q", t=PLANES))
+        nc.sync.dma_start(key_planes[LAST][:], key_rows[LAST])
         nc.sync.dma_start(list_out[:], offs4)
         nc.sync.dma_start(fade_sb[:], fade)
         nc.sync.dma_start(old_sb[:], old)
@@ -63,67 +74,65 @@ def tile_attend_keymiddle_counts_lean_kernel(tc, query, keys, old, fade, offs, o
         wf = sb.tile([P, M], F32, name="wf")
         nc.vector.memset(wf[:], 0.0)
 
-        lo = sb.tile([P, PACK, I], F32, name="lo")
-        mid = sb.tile([P, PACK, I], F32, name="mid")
+        lo = sb.tile([P, PLANES, I], F32, name="lo")
+        capped = sb.tile([P, PLANES, I], F32, name="capped", tag="capped")
 
-        def gather(on_vector, dst, t, offsets, first, count):
-            src = planes[t][:].indirect(entries(offsets, first, count))
-            if on_vector:
-                nc.vector.tensor_copy(dst, src)
-            else:
-                nc.scalar.activation(dst, src, ACT.Copy)
+        def picked(t, offsets, first, count):
+            return key_planes[t][:].indirect(entries(offsets, first, count))
 
-        for t in range(PACK - 1):
+        for t, on_vector in enumerate(VECTOR_SLOTS):
             a = sb.tile([P, I], F32, name=f"a{t}")
             b = sb.tile([P, I], F32, name=f"b{t}")
             c = sb.tile([P, I], F32, name=f"c{t}")
             hi = sb.tile([P, I], F32, name=f"hi{t}")
-            gather(False, a[:], t, list_a, 0, I)
-            share = VECTOR_SHARE_OF_B[t]
-            if share:
-                gather(True, b[:, :share], t, list_b, 0, share)
-            if share < I:
-                gather(False, b[:, share:], t, list_b, share, I - share)
-            gather(False, c[:], t, list_c, 0, I)
+            nc.scalar.activation(a[:], picked(t, list_a, 0, I), ACT.Copy)
+            nc.vector.tensor_copy(b[:, :on_vector], picked(t, list_b, 0, on_vector))
+            if on_vector < I:
+                nc.scalar.activation(b[:, on_vector:], picked(t, list_b, on_vector, I - on_vector), ACT.Copy)
+            nc.scalar.activation(c[:], picked(t, list_c, 0, I), ACT.Copy)
             nc.vector.tensor_tensor(hi[:], a[:], b[:], ALU.max)
             nc.vector.tensor_tensor(lo[:, t, :], a[:], b[:], ALU.min)
-            nc.vector.tensor_tensor(mid[:, t, :], hi[:], c[:], ALU.min)
+            nc.vector.tensor_tensor(capped[:, t, :], hi[:], c[:], ALU.min)
 
-        last = PACK - 1
-        halves = [slice(0, HALF), slice(HALF, I)]
-        abc = [[sb.tile([P, HALF], F32, name=f"{x}_last{h}") for x in "abc"] for h in range(2)]
-        hi_first = sb.tile([P, HALF], F32, name="hi_first")
-        his = [hi_first[:], sb.tile([P, HALF], F32, name="hi_second")[:]]
+        q_bf = sb.tile([P, Q, PLANES], BF16, name="q_bf", align_bytes=64)
+        q_codes = sb.tile([P, Q], U32, name="q_codes", align_bytes=64)
+        q_scales = sb.tile([P, Q], U8, name="q_scales", align_bytes=64)
+        nc.vector.tensor_copy(words_in_runs(q_bf[:]), planes_in_runs(q_planes[:]))
+        nc.vector.quantize_mx(q_codes[:].bitcast(FP8X4), q_scales[:], q_bf[:].rearrange("p q t -> p (q t)"))
 
-        def gathers(h):
-            for dst, offsets in zip(abc[h], (list_a, list_b, list_c)):
-                gather(False, dst[:], last, offsets, h * HALF, HALF)
+        def quarter(j):
+            return slice(j * QUARTER, (j + 1) * QUARTER)
 
-        def upper(h):
-            nc.vector.tensor_tensor(his[h], abc[h][0][:], abc[h][1][:], ALU.max)
+        hi_last = [sb.tile([P, QUARTER], F32, name=f"hi_last{j}") for j in range(QUARTERS)]
+        abc_last = [[sb.tile([P, QUARTER], F32, name=f"{x}_last{j}") for x in "abc"] for j in range(QUARTERS)]
+        for j in range(QUARTERS):
+            for dst, offsets in zip(abc_last[j], (list_a, list_b, list_c)):
+                nc.scalar.activation(dst[:], picked(LAST, offsets, j * QUARTER, QUARTER), ACT.Copy)
 
-        def lower(h):
-            nc.vector.tensor_tensor(lo[:, last, halves[h]], abc[h][0][:], abc[h][1][:], ALU.min)
+        def upper(j):
+            nc.vector.tensor_tensor(hi_last[j][:], abc_last[j][0][:], abc_last[j][1][:], ALU.max)
 
-        def cap(h):
-            nc.vector.tensor_tensor(mid[:, last, halves[h]], his[h], abc[h][2][:], ALU.min)
+        def lower(j):
+            nc.vector.tensor_tensor(lo[:, LAST, quarter(j)], abc_last[j][0][:], abc_last[j][1][:], ALU.min)
 
-        def middle(first, count):
-            zk = sb.tile([P, count, PACK], BF16, name=f"zk{first}", align_bytes=64)
-            span = slice(first, first + count)
+        def cap(j):
+            nc.vector.tensor_tensor(capped[:, LAST, quarter(j)], hi_last[j][:], abc_last[j][2][:], ALU.min)
+
+        def middle(j):
+            zk = sb.tile([P, QUARTER, PLANES], BF16, name=f"zk{j}", align_bytes=64)
             nc.vector.tensor_tensor(
-                zk[:].rearrange("p (c i) t -> p c t i", i=LINE),
-                lo[:, :, span].rearrange("p t (c i) -> p c t i", i=LINE),
-                mid[:, :, span].rearrange("p t (c i) -> p c t i", i=LINE),
+                words_in_runs(zk[:]),
+                planes_in_runs(lo[:, :, quarter(j)]),
+                planes_in_runs(capped[:, :, quarter(j)]),
                 ALU.max,
             )
             return zk
 
-        def score(zk, first, count):
-            codes = sb.tile([P, count], U32, name=f"k_codes{first}", align_bytes=64)
-            scales = sb.tile([P, count], U8, name=f"k_scales{first}", align_bytes=64)
+        def score(j, zk):
+            codes = sb.tile([P, QUARTER], U32, name=f"k_codes{j}", align_bytes=64)
+            scales = sb.tile([P, QUARTER], U8, name=f"k_scales{j}", align_bytes=64)
             nc.vector.quantize_mx(codes[:].bitcast(FP8X4), scales[:], zk[:].rearrange("p i t -> p (i t)"))
-            s = ps.tile([P, count], F32, name=f"s{first}")
+            s = ps.tile([P, QUARTER], F32, name=f"s{j}")
             nc.tensor.matmul_mx(
                 s[:],
                 lhsT=q_codes[:].bitcast(FP8X4),
@@ -135,34 +144,30 @@ def tile_attend_keymiddle_counts_lean_kernel(tc, query, keys, old, fade, offs, o
             )
             return s
 
-        gathers(0)
-        q_bf = sb.tile([P, Q, PACK], BF16, name="q_bf", align_bytes=64)
-        q_codes = sb.tile([P, Q], U32, name="q_codes", align_bytes=64)
-        q_scales = sb.tile([P, Q], U8, name="q_scales", align_bytes=64)
-        nc.scalar.copy(
-            q_bf[:].rearrange("p (c i) t -> p c t i", i=LINE),
-            q_raw[:].rearrange("p t (c i) -> p c t i", i=LINE),
-        )
-        gathers(1)
+        w_first = sb.tile([P, HALF], F32, name="w_first")
+        scores = []
         upper(0)
         lower(0)
         cap(0)
-        nc.vector.quantize_mx(q_codes[:].bitcast(FP8X4), q_scales[:], q_bf[:].rearrange("p q t -> p (q t)"))
-        zk_first = middle(0, HALF)
-        upper(1)
-        s_first = score(zk_first, 0, HALF)
-        w_first = sb.tile([P, HALF], F32, name="w_first")
-        nc.scalar.activation(w_first[:], s_first[:], ACT.Sigmoid)
-        nc.scalar.activation(wf[:].indirect(entries(list_out, 0, HALF)), w_first[:], ACT.Copy, scale=2.0)
-        lower(1)
-        cap(1)
-        quarters = (HALF, HALF + QUARTER)
-        zks = [middle(first, QUARTER) for first in quarters]
-        scores = [score(zk, first, QUARTER) for zk, first in zip(zks, quarters)]
-        for s, first in zip(scores, quarters):
-            w = sb.tile([P, QUARTER], F32, name=f"w{first}")
-            nc.scalar.activation(w[:], s[:], ACT.Sigmoid)
-            nc.vector.tensor_tensor(wf[:].indirect(entries(list_out, first, QUARTER)), w[:], w[:], ALU.add)
+        for j in range(QUARTERS):
+            more = j + 1 < QUARTERS
+            if more:
+                upper(j + 1)
+            zk = middle(j)
+            if more:
+                lower(j + 1)
+            scores.append(score(j, zk))
+            if more:
+                cap(j + 1)
+            if j < QUARTERS // 2:
+                nc.scalar.activation(w_first[:, quarter(j)], scores[j][:], ACT.Sigmoid)
+            if j == QUARTERS // 2 - 1:
+                nc.scalar.activation(wf[:].indirect(entries(list_out, 0, HALF)), w_first[:], ACT.Copy, scale=2.0)
+
+        for j, tag in ((2, "capped"), (3, "w_last")):
+            w = sb.tile([P, QUARTER], F32, name=f"w{j}", tag=tag)
+            nc.scalar.activation(w[:], scores[j][:], ACT.Sigmoid)
+            nc.vector.tensor_tensor(wf[:].indirect(entries(list_out, j * QUARTER, QUARTER)), w[:], w[:], ALU.add)
 
         first = 0
         for n, width in enumerate(STORE_WIDTHS):

from contextlib import ExitStack

import concourse.mybir as mybir

D, T, I, Q, M = 512, 2048, 512, 128, 2048
FLOPS = 2 * D * Q * I

F32 = mybir.dt.float32
BF16 = mybir.dt.bfloat16
U32 = mybir.dt.uint32
U16 = mybir.dt.uint16
U8 = mybir.dt.uint8
FP8X4 = mybir.dt.float8_e4m3fn_x4
ALU = mybir.AluOpType
ACT = mybir.ActivationFunctionType

P = 128
PLANES = 4
LAST = PLANES - 1
RUN = 4
PER_COLUMN = 16
HALF = I // 2
QUARTERS = 4
QUARTER = I // QUARTERS
VECTOR_SLOTS = (512, 512, 256)
STORE_WIDTHS = (256, 512, 512, 384, 256, 128)


def entries(offsets, first, count):
    return offsets[:, first // PER_COLUMN : (first + count) // PER_COLUMN]


def planes_in_runs(planes):
    return planes.rearrange("p t (c i) -> p c t i", i=RUN)


def words_in_runs(words):
    return words.rearrange("p (c i) t -> p c t i", i=RUN)


def tile_attend_keymiddle_counts_lean_kernel(tc, query, keys, old, fade, offs, offs2, offs3, offs4, out):
    nc = tc.nc
    with ExitStack() as ctx:
        sb = ctx.enter_context(tc.tile_pool(name="sb", bufs=1))
        ps = ctx.enter_context(tc.psum_pool(name="ps", bufs=1))

        list_a = sb.tile([P, I // PER_COLUMN], U16, name="list_a")
        list_b = sb.tile([P, I // PER_COLUMN], U16, name="list_b")
        list_c = sb.tile([P, I // PER_COLUMN], U16, name="list_c")
        list_out = sb.tile([P, I // PER_COLUMN], U16, name="list_out")
        key_planes = [sb.tile([P, T], F32, name=f"key_plane{t}") for t in range(PLANES)]
        key_rows = keys.rearrange("(p t) n -> t p n", t=PLANES)
        q_planes = sb.tile([P, PLANES, Q], F32, name="q_planes")
        old_sb = sb.tile([P, M], F32, name="old_sb")
        fade_sb = sb.tile([P, 1], F32, name="fade_sb")

        nc.sync.dma_start(key_planes[0][:], key_rows[0])
        nc.sync.dma_start(list_a[:], offs)
        nc.sync.dma_start(list_b[:], offs2)
        nc.sync.dma_start(list_c[:], offs3)
        for t in range(1, LAST):
            nc.sync.dma_start(key_planes[t][:], key_rows[t])
        nc.sync.dma_start(q_planes[:], query.rearrange("(p t) q -> p t q", t=PLANES))
        nc.sync.dma_start(key_planes[LAST][:], key_rows[LAST])
        nc.sync.dma_start(list_out[:], offs4)
        nc.sync.dma_start(fade_sb[:], fade)
        nc.sync.dma_start(old_sb[:], old)

        warm_in = sb.tile([P, 1], F32, name="warm_in")
        warm_out = sb.tile([P, 1], F32, name="warm_out")
        nc.vector.memset(warm_in[:], 0.0)
        nc.scalar.activation(warm_out[:], warm_in[:], ACT.Sigmoid)

        wf = sb.tile([P, M], F32, name="wf")
        nc.vector.memset(wf[:], 0.0)

        lo = sb.tile([P, PLANES, I], F32, name="lo")
        capped = sb.tile([P, PLANES, I], F32, name="capped", tag="capped")

        def picked(t, offsets, first, count):
            return key_planes[t][:].indirect(entries(offsets, first, count))

        for t, on_vector in enumerate(VECTOR_SLOTS):
            a = sb.tile([P, I], F32, name=f"a{t}")
            b = sb.tile([P, I], F32, name=f"b{t}")
            c = sb.tile([P, I], F32, name=f"c{t}")
            hi = sb.tile([P, I], F32, name=f"hi{t}")
            nc.scalar.activation(a[:], picked(t, list_a, 0, I), ACT.Copy)
            nc.vector.tensor_copy(b[:, :on_vector], picked(t, list_b, 0, on_vector))
            if on_vector < I:
                nc.scalar.activation(b[:, on_vector:], picked(t, list_b, on_vector, I - on_vector), ACT.Copy)
            nc.scalar.activation(c[:], picked(t, list_c, 0, I), ACT.Copy)
            nc.vector.tensor_tensor(hi[:], a[:], b[:], ALU.max)
            nc.vector.tensor_tensor(lo[:, t, :], a[:], b[:], ALU.min)
            nc.vector.tensor_tensor(capped[:, t, :], hi[:], c[:], ALU.min)

        q_bf = sb.tile([P, Q, PLANES], BF16, name="q_bf", align_bytes=64)
        q_codes = sb.tile([P, Q], U32, name="q_codes", align_bytes=64)
        q_scales = sb.tile([P, Q], U8, name="q_scales", align_bytes=64)
        nc.vector.tensor_copy(words_in_runs(q_bf[:]), planes_in_runs(q_planes[:]))
        nc.vector.quantize_mx(q_codes[:].bitcast(FP8X4), q_scales[:], q_bf[:].rearrange("p q t -> p (q t)"))

        def quarter(j):
            return slice(j * QUARTER, (j + 1) * QUARTER)

        hi_last = [sb.tile([P, QUARTER], F32, name=f"hi_last{j}") for j in range(QUARTERS)]
        abc_last = [[sb.tile([P, QUARTER], F32, name=f"{x}_last{j}") for x in "abc"] for j in range(QUARTERS)]
        for j in range(QUARTERS):
            for dst, offsets in zip(abc_last[j], (list_a, list_b, list_c)):
                nc.scalar.activation(dst[:], picked(LAST, offsets, j * QUARTER, QUARTER), ACT.Copy)

        def upper(j):
            nc.vector.tensor_tensor(hi_last[j][:], abc_last[j][0][:], abc_last[j][1][:], ALU.max)

        def lower(j):
            nc.vector.tensor_tensor(lo[:, LAST, quarter(j)], abc_last[j][0][:], abc_last[j][1][:], ALU.min)

        def cap(j):
            nc.vector.tensor_tensor(capped[:, LAST, quarter(j)], hi_last[j][:], abc_last[j][2][:], ALU.min)

        def middle(j):
            zk = sb.tile([P, QUARTER, PLANES], BF16, name=f"zk{j}", align_bytes=64)
            nc.vector.tensor_tensor(
                words_in_runs(zk[:]),
                planes_in_runs(lo[:, :, quarter(j)]),
                planes_in_runs(capped[:, :, quarter(j)]),
                ALU.max,
            )
            return zk

        def score(j, zk):
            codes = sb.tile([P, QUARTER], U32, name=f"k_codes{j}", align_bytes=64)
            scales = sb.tile([P, QUARTER], U8, name=f"k_scales{j}", align_bytes=64)
            nc.vector.quantize_mx(codes[:].bitcast(FP8X4), scales[:], zk[:].rearrange("p i t -> p (i t)"))
            s = ps.tile([P, QUARTER], F32, name=f"s{j}")
            nc.tensor.matmul_mx(
                s[:],
                lhsT=q_codes[:].bitcast(FP8X4),
                lhsT_scale=q_scales[:],
                rhs=codes[:].bitcast(FP8X4),
                rhs_scale=scales[:],
                start=True,
                stop=True,
            )
            return s

        w_first = sb.tile([P, HALF], F32, name="w_first")
        scores = []
        upper(0)
        lower(0)
        cap(0)
        for j in range(QUARTERS):
            more = j + 1 < QUARTERS
            if more:
                upper(j + 1)
            zk = middle(j)
            if more:
                lower(j + 1)
            scores.append(score(j, zk))
            if more:
                cap(j + 1)
            if j < QUARTERS // 2:
                nc.scalar.activation(w_first[:, quarter(j)], scores[j][:], ACT.Sigmoid)
            if j == QUARTERS // 2 - 1:
                nc.scalar.activation(wf[:].indirect(entries(list_out, 0, HALF)), w_first[:], ACT.Copy, scale=2.0)

        for j, tag in ((2, "capped"), (3, "w_last")):
            w = sb.tile([P, QUARTER], F32, name=f"w{j}", tag=tag)
            nc.scalar.activation(w[:], scores[j][:], ACT.Sigmoid)
            nc.vector.tensor_tensor(wf[:].indirect(entries(list_out, j * QUARTER, QUARTER)), w[:], w[:], ALU.add)

        first = 0
        for n, width in enumerate(STORE_WIDTHS):
            span = slice(first, first + width)
            res = sb.tile([P, width], F32, name=f"res{n}")
            nc.vector.scalar_tensor_tensor(res[:], old_sb[:, span], fade_sb[:], wf[:, span], ALU.mult, ALU.add)
            queue = nc.sync if n % 2 == 0 else nc.scalar
            queue.dma_start(out[:, span], res[:])
            first = first + width
